import numpy as np
import ml_dtypes


def mxq(x, axis, fmt="e4m3"):
    dtype, down = {"e4m3": (ml_dtypes.float8_e4m3fn, 7), "e5m2": (ml_dtypes.float8_e5m2, 14)}[fmt]
    v = np.moveaxis(np.asarray(x, np.float32).astype(ml_dtypes.bfloat16).astype(np.float64), axis, -1)
    blocks = v.reshape(v.shape[:-1] + (-1, 32))
    amax = np.abs(blocks).max(-1, keepdims=True)
    byte = np.maximum(np.where(amax > 0, np.frexp(amax)[1] - 1 + 127, 0) - down, 1)
    scale = np.exp2(byte - 127.0)
    codes = (blocks / scale).astype(np.float32).astype(dtype).astype(np.float64)
    return np.moveaxis((codes * scale).reshape(v.shape), -1, axis)


WIDE = False


def mx_kscale(k):
    if not WIDE:
        return np.ones(k)
    levels = np.array([10, -10, 5, -5, 0])
    if k % 512:
        return np.exp2(np.random.permutation(np.resize(levels, k // 32))).repeat(32)
    a = np.empty((k // 512, 16))
    for p in range(k // 512):
        a[p, :8] = np.random.permutation(np.resize(levels, 8))
        for g in range(8):
            far = levels[np.abs(levels - a[p, g]) >= 10]
            a[p, g + 8] = far[np.random.randint(len(far))]
    return np.exp2(a.ravel()).repeat(32)


def f64(x):
    return np.asarray(x).astype(np.float64)


def striped(idx):
    return np.tile(idx.reshape(-1, 16).T, (8, 1)).astype(np.uint16)


def unstriped(offs):
    return offs[:16].T.reshape(-1).astype(np.int64)


def pack_weight(w):
    k, n = w.shape
    w = f64(np.asarray(w, np.float32).astype(ml_dtypes.bfloat16)).reshape(k // 32, 32, n)
    amax = np.abs(w).max(1)
    byte = np.clip(np.where(amax > 0, np.frexp(amax)[1] - 1 + 127 - 7, 1), 1, 254)
    scaled = (w * np.exp2(127.0 - byte)[:, None, :]).reshape(k, n).astype(np.float32)
    words = np.ascontiguousarray(scaled.reshape(k // 512, 128, 4, n).transpose(0, 1, 3, 2)).astype(ml_dtypes.float8_e4m3fn).view(np.uint8)
    return words, np.ascontiguousarray(byte.astype(np.uint8).reshape(k // 512, 16, n))


def unpack_weight(words, scales):
    g, p, n, _ = words.shape
    vals = np.ascontiguousarray(words).view(ml_dtypes.float8_e4m3fn).astype(np.float64) * np.repeat(np.exp2(scales.astype(np.float64) - 127.0), 8, axis=1)[..., None]
    return vals.transpose(0, 1, 3, 2).reshape(g * 512, n)

def planes(y):
    n, m = y.shape
    v = y.astype(np.float32).astype(ml_dtypes.bfloat16).astype(np.float64).reshape(n // 32, 32, m)
    top = np.abs(v).max(1)
    byte = np.clip(np.where(top > 0, np.frexp(top)[1] - 1 + 127 - 7, 1), 1, 254)
    codes = (v * np.exp2(127.0 - byte)[:, None, :]).reshape(n, m).astype(np.float32).astype(ml_dtypes.float8_e4m3fn).view(np.uint8)
    words = codes.reshape(n // 512, 128, 4, m).transpose(0, 1, 3, 2)
    return np.ascontiguousarray(words), np.ascontiguousarray(byte.astype(np.uint8).reshape(n // 512, 16, m))


K, T, S, N, W = 512, 2048, 256, 512, 128


def setup_inputs():
    n = np.random.standard_normal
    s = mx_kscale(K)[:, None]
    packed_xT = pack_weight(n((K, T)) * s)
    perm = np.random.permutation(S)
    return {
        "x_words": packed_xT[0],
        "x_scales": packed_xT[1],
        "w1": (n((K, N)) / np.sqrt(2 * K) / s).astype(np.float32),
        "w2": (n((K, N)) / np.sqrt(2 * K) / s).astype(np.float32),
        "offs": striped(np.random.permutation(T)[:S]),
        "two": striped(np.random.permutation(T)[:S]),
        "n1": striped(perm[:W]),
        "n2": striped(perm[W:]),
    }


def reference(x_words, x_scales, w1, w2, offs, two, n1, n2):
    xq = unpack_weight(x_words, x_scales)[:, unstriped(offs)]
    x_two = unpack_weight(x_words, x_scales)[:, unstriped(two)]
    h = mxq(f64(w1), 0, "e4m3").T @ xq + mxq(f64(w2), 0, "e4m3").T @ x_two
    pb = h[:, unstriped(n2)]
    pa = h[:, unstriped(n1)]
    rb = pb - (0.5 * pa)
    ra = np.sqrt((pa) ** 2 + (pb) ** 2 + 0.25)
    ds = np.zeros((N, S))
    ds[:, unstriped(n1)] = ra
    out = ds.copy()
    out[:, unstriped(n2)] = rb
    return (out,) + planes(out)

@@ -1,0 +1,257 @@
+from contextlib import ExitStack
+
+import concourse.mybir as mybir
+
+K, T, S, N, W = 512, 2048, 256, 512, 128
+FLOPS = 2 * 2 * K * N * S
+
+F32 = mybir.dt.float32
+BF16 = mybir.dt.bfloat16
+I32 = mybir.dt.int32
+U32 = mybir.dt.uint32
+U16 = mybir.dt.uint16
+U8 = mybir.dt.uint8
+FP8X4 = mybir.dt.float8_e4m3fn_x4
+ACT = mybir.ActivationFunctionType
+ALU = mybir.AluOpType
+
+P = 128
+HALF = 64
+
+
+def tile_picked_ottpolar_none_po_kernel(tc, x_words, x_scales, w1, w2, offs, two, n1, n2, out_0, out_1, out_2):
+    nc = tc.nc
+    with ExitStack() as ctx:
+        lists = ctx.enter_context(tc.tile_pool(name="lists", bufs=1))
+        sb = ctx.enter_context(tc.tile_pool(name="sb", bufs=1))
+        psum = ctx.enter_context(tc.psum_pool(name="psum", bufs=1))
+
+        def load_list(name, src):
+            tile = lists.tile(list(src.shape), U16, name="list_" + name)
+            nc.sync.dma_start(tile[:], src)
+            return tile
+
+        raw = {}
+
+        def load_weight(i, c):
+            raw[i, c] = sb.tile([P, 4, 256], F32, name="raw%d%d" % (i, c), align_bytes=64)
+            nc.sync.dma_start(raw[i, c][:], (w1, w2)[i].rearrange("(p j) n -> p j n", j=4)[:, :, 256 * c : 256 * (c + 1)])
+
+        xs = sb.tile([P, T], U8, name="xs", align_bytes=64)
+        xw = sb.tile([P, T], I32, name="xw", align_bytes=64)
+        nc.vector.memset(xs[:].bitcast(I32), 0)
+
+        def load_words():
+            nc.sync.dma_start(xw[:], x_words[0].rearrange("p n t -> p (n t)").bitcast(I32))
+
+        def load_scales(queues):
+            for q in range(4):
+                queues[q].dma_start(xs[32 * q : 32 * q + 4, :].bitcast(I32), x_scales[0, 4 * q : 4 * q + 4, :].bitcast(I32))
+
+        l_offs = load_list("offs", offs)
+        l_two = load_list("two", two)
+        load_words()
+        load_scales([nc.sync] * 4)
+        load_weight(0, 0)
+        load_weight(1, 0)
+        load_weight(0, 1)
+        l_n1 = load_list("n1", n1)
+        l_n2 = load_list("n2", n2)
+        load_weight(1, 1)
+
+        gw = [sb.tile([P, S], U32, name="gw%d" % i, align_bytes=64) for i in range(2)]
+        gs = [sb.tile([P, S], U8, name="gs%d" % i, align_bytes=64) for i in range(2)]
+
+        def pick_words(i):
+            nc.vector.tensor_copy(gw[i][:], xw[:].bitcast(U32).indirect((l_offs, l_two)[i][:]))
+
+        def pick_scales(i):
+            nc.vector.tensor_copy(gs[i][:], xs[:].indirect((l_offs, l_two)[i][:]))
+
+        g01 = {(i, c): sb.tile([P, 512], BF16, name="g01_%d%d" % (i, c), align_bytes=64) for i in range(2) for c in range(2)}
+        g23 = [sb.tile([P, 1024], BF16, name="g23_%d" % i, align_bytes=64) for i in range(2)]
+        w01 = {(i, c): sb.tile([P, 128], U32, name="w01_%d%d" % (i, c), align_bytes=64) for i in range(2) for c in range(2)}
+        s01 = {(i, c): sb.tile([P, 128], U8, name="s01_%d%d" % (i, c), align_bytes=64) for i in range(2) for c in range(2)}
+        w23 = [sb.tile([P, 256], U32, name="w23_%d" % i, align_bytes=64) for i in range(2)]
+        s23 = [sb.tile([P, 256], U8, name="s23_%d" % i, align_bytes=64) for i in range(2)]
+
+        def cast01(copy, i, c):
+            copy(g01[i, c][:].rearrange("p (t m j) -> p m j t", t=2, j=4),
+                 raw[i, c][:].rearrange("p j (m t) -> p m j t", t=4)[:, :, :, 0:2])
+
+        def cast23(copy, i, c):
+            copy(g23[i][:].rearrange("p (t c m j) -> p c m j t", t=2, c=2, j=4)[:, c],
+                 raw[i, c][:].rearrange("p j (m t) -> p m j t", t=4)[:, :, :, 2:4])
+
+        def quant01(i, c):
+            nc.vector.quantize_mx(out=w01[i, c][:].bitcast(FP8X4), scales=s01[i, c][:], in_=g01[i, c][:])
+
+        def quant23(i):
+            nc.vector.quantize_mx(out=w23[i][:].bitcast(FP8X4), scales=s23[i][:], in_=g23[i][:])
+
+        banks = [psum.tile([P, S], F32, name="bank%d" % u) for u in range(4)]
+
+        def product(u, i):
+            if u < 2:
+                words, scales = w01[i, u][:], s01[i, u][:]
+            else:
+                cols = slice(128 * (u - 2), 128 * (u - 1))
+                words, scales = w23[i][:, cols], s23[i][:, cols]
+            nc.tensor.matmul_mx(out=banks[u][:], lhsT=words.bitcast(FP8X4), lhsT_scale=scales,
+                                rhs=gw[i][:].bitcast(FP8X4), rhs_scale=gs[i][:], start=(i == 0), stop=(i == 1))
+
+        h = {}
+        y = {}
+        pa_pb, rb, ss, ra = {}, {}, {}, {}
+        groups = {0: (0,), 1: (1,), 2: (2, 3)}
+        for g, members in groups.items():
+            n = len(members)
+            pa_pb[g] = sb.tile([P, 2, n * W], F32, name="pair%d" % g, align_bytes=64)
+            rb[g] = sb.tile([P, n * W], F32, name="rb%d" % g, align_bytes=64)
+            ss[g] = sb.tile([P, n * W], F32, name="ss%d" % g, tag="ss%d" % g, align_bytes=64)
+
+        def place(u):
+            g = min(u, 2)
+            return g, slice(W * (u - g), W * (u - g + 1))
+
+        def unload(copy, u):
+            h[u] = sb.tile([P, S], F32, name="h%d" % u, tag="h%d" % u, align_bytes=64)
+            copy(h[u][:], banks[u][:])
+
+        def fetch(u):
+            g, cols = place(u)
+            nc.scalar.activation(pa_pb[g][:, 0, cols], h[u][:].indirect(l_n1[:]), ACT.Copy)
+            nc.scalar.activation(pa_pb[g][:, 1, cols], h[u][:].indirect(l_n2[:]), ACT.Copy)
+
+        def open_y(u, tag):
+            y[u] = sb.tile([P, S], F32, name="y%d" % u, tag=tag, align_bytes=64)
+
+        def fetch_half(u, a):
+            cols, offsets = slice(HALF * a, HALF * (a + 1)), slice(4 * a, 4 * (a + 1))
+            nc.scalar.activation(pa_pb[u][:, 0, cols], h[u][:].indirect(l_n1[:, offsets]), ACT.Copy)
+            nc.scalar.activation(pa_pb[u][:, 1, cols], h[u][:].indirect(l_n2[:, offsets]), ACT.Copy)
+
+        def make_rb_half(u, a):
+            cols = slice(HALF * a, HALF * (a + 1))
+            nc.vector.scalar_tensor_tensor(rb[u][:, cols], pa_pb[u][:, 0, cols], -0.5, pa_pb[u][:, 1, cols], ALU.mult, ALU.add)
+
+        def put_rb_half(u, a):
+            cols, offsets = slice(HALF * a, HALF * (a + 1)), slice(4 * a, 4 * (a + 1))
+            nc.scalar.activation(y[u][:].indirect(l_n2[:, offsets]), rb[u][:, cols], ACT.Copy)
+
+        def make_rb(u):
+            g, cols = place(u)
+            nc.vector.scalar_tensor_tensor(rb[g][:, cols], pa_pb[g][:, 0, cols], -0.5, pa_pb[g][:, 1, cols], ALU.mult, ALU.add)
+
+        sq = {g: sb.tile(list(pa_pb[g].shape), F32, name="sq%d" % g, align_bytes=64) for g in groups}
+
+        def make_sq(u):
+            g, cols = place(u)
+            nc.vector.tensor_tensor(sq[g][:, :, cols], pa_pb[g][:, :, cols], pa_pb[g][:, :, cols], ALU.mult)
+
+        def make_ss(g):
+            nc.vector.scalar_tensor_tensor(ss[g][:], sq[g][:, 0, :], 0.25, sq[g][:, 1, :], ALU.add, ALU.add)
+
+        def root(g, tag):
+            ra[g] = sb.tile(list(ss[g].shape), F32, name="ra%d" % g, tag=tag, align_bytes=64)
+            nc.scalar.activation(ra[g][:], ss[g][:], ACT.Sqrt)
+
+        def put_rb(u):
+            g, cols = place(u)
+            nc.scalar.activation(y[u][:].indirect(l_n2[:]), rb[g][:, cols], ACT.Copy)
+
+        def put_ra(u):
+            g, cols = place(u)
+            nc.scalar.activation(y[u][:].indirect(l_n1[:]), ra[g][:, cols], ACT.Copy)
+
+        y01 = sb.tile([P, 2, S], F32, name="y01", align_bytes=64)
+        grouped = sb.tile([P, S, 4], BF16, name="grouped", align_bytes=64)
+        out_rows = out_0.rearrange("(p t) c -> p t c", t=4)
+
+        def regroup(u):
+            for t in range(2):
+                nc.sync.dma_start(y01[HALF * u : HALF * (u + 1), t, :], y[u][HALF * t : HALF * (t + 1), :])
+
+        vcopy, scopy = nc.vector.tensor_copy, nc.scalar.copy
+        pick_words(0)
+        pick_words(1)
+        pick_scales(0)
+        pick_scales(1)
+        cast01(scopy, 0, 0)
+        cast23(scopy, 0, 0)
+        quant01(0, 0)
+        cast01(vcopy, 1, 0)
+        quant01(1, 0)
+        cast23(scopy, 1, 0)
+        product(0, 0)
+        product(0, 1)
+        unload(scopy, 0)
+        cast01(vcopy, 0, 1)
+        cast23(vcopy, 0, 1)
+        quant01(0, 1)
+        quant23(0)
+        fetch_half(0, 0)
+        fetch_half(0, 1)
+        make_rb_half(0, 0)
+        cast01(vcopy, 1, 1)
+        make_rb_half(0, 1)
+        open_y(0, "y0")
+        put_rb_half(0, 0)
+        put_rb_half(0, 1)
+        make_sq(0)
+        quant01(1, 1)
+        make_ss(0)
+        product(1, 0)
+        product(1, 1)
+        root(0, "ra0")
+        put_ra(0)
+        regroup(0)
+        cast23(vcopy, 1, 1)
+        unload(vcopy, 1)
+        quant23(1)
+        product(2, 0)
+        product(2, 1)
+        product(3, 0)
+        product(3, 1)
+        unload(vcopy, 2)
+        fetch_half(1, 0)
+        fetch_half(1, 1)
+        make_rb_half(1, 0)
+        unload(vcopy, 3)
+        make_rb_half(1, 1)
+        open_y(1, "y1")
+        put_rb_half(1, 0)
+        put_rb_half(1, 1)
+        make_sq(1)
+        make_ss(1)
+        fetch(2)
+        root(1, "h2")
+        fetch(3)
+        make_rb(2)
+        make_sq(2)
+        put_ra(1)
+        regroup(1)
+        make_sq(3)
+        make_rb(3)
+        make_ss(2)
+        open_y(2, "h2")
+        put_rb(2)
+        root(2, "ra2")
+        open_y(3, "ss2")
+        put_rb(3)
+        put_ra(2)
+        nc.sync.dma_start(out_rows[:, 0:2, :], y01[:])
+        vcopy(grouped[:, :, 0:2], y01[:].rearrange("p t c -> p c t"))
+        nc.sync.dma_start(out_rows[:, 2, :], y[2][:])
+        vcopy(grouped[:, :, 2], y[2][:])
+        put_ra(3)
+        nc.sync.dma_start(out_rows[:, 3, :], y[3][:])
+        vcopy(grouped[:, :, 3], y[3][:])
+
+        yw = sb.tile([P, S], U32, name="yw", align_bytes=64)
+        ys = sb.tile([P, S], U8, name="ys", align_bytes=64)
+        nc.vector.quantize_mx(out=yw[:].bitcast(FP8X4), scales=ys[:], in_=grouped[:].rearrange("p c t -> p (c t)"))
+        nc.sync.dma_start(out_1[0].rearrange("p n t -> p (n t)").bitcast(I32), yw[:].bitcast(I32))
+        for q in range(4):
+            queue = nc.scalar if q % 2 == 0 else nc.sync
+            queue.dma_start(out_2[0, 4 * q : 4 * q + 4, :].bitcast(I32), ys[32 * q : 32 * q + 4, :].bitcast(I32))

@@ -40,6 +40,9 @@ def tile_picked_ottpolar_none_po_kernel(tc, x_words, x_scales, w1, w2, offs, two
         xs = sb.tile([P, T], U8, name="xs", align_bytes=64)
         xw = sb.tile([P, T], I32, name="xw", align_bytes=64)
         nc.vector.memset(xs[:].bitcast(I32), 0)
+        warm = sb.tile([P, 2], F32, name="warm")
+        nc.gpsimd.memset(warm[:, 0:1], 1.0)
+        nc.scalar.activation(warm[:, 1:2], warm[:, 0:1], ACT.Sqrt)
 
         def load_words():
             nc.sync.dma_start(xw[:], x_words[0].rearrange("p n t -> p (n t)").bitcast(I32))

@@ -51,9 +51,9 @@ def tile_picked_ottpolar_none_po_kernel(tc, x_words, x_scales, w1, w2, offs, two
             for q in range(4):
                 queues[q].dma_start(xs[32 * q : 32 * q + 4, :].bitcast(I32), x_scales[0, 4 * q : 4 * q + 4, :].bitcast(I32))
 
+        load_words()
         l_offs = load_list("offs", offs)
         l_two = load_list("two", two)
-        load_words()
         load_scales([nc.sync] * 4)
         load_weight(0, 0)
         load_weight(1, 0)
@@ -79,12 +79,12 @@ def tile_picked_ottpolar_none_po_kernel(tc, x_words, x_scales, w1, w2, offs, two
         s23 = [sb.tile([P, 256], U8, name="s23_%d" % i, align_bytes=64) for i in range(2)]
 
         def cast01(copy, i, c):
-            copy(g01[i, c][:].rearrange("p (t m j) -> p m j t", t=2, j=4),
-                 raw[i, c][:].rearrange("p j (m t) -> p m j t", t=4)[:, :, :, 0:2])
+            copy(g01[i, c][:].rearrange("p (m t j) -> p m t j", t=2, j=4),
+                 raw[i, c][:].rearrange("p j (m t) -> p m t j", t=4)[:, :, 0:2, :])
 
         def cast23(copy, i, c):
-            copy(g23[i][:].rearrange("p (t c m j) -> p c m j t", t=2, c=2, j=4)[:, c],
-                 raw[i, c][:].rearrange("p j (m t) -> p m j t", t=4)[:, :, :, 2:4])
+            copy(g23[i][:].rearrange("p (t c m j) -> p c m t j", t=2, c=2, j=4)[:, c],
+                 raw[i, c][:].rearrange("p j (m t) -> p m t j", t=4)[:, :, 2:4, :])
 
         def quant01(i, c):
             nc.vector.quantize_mx(out=w01[i, c][:].bitcast(FP8X4), scales=s01[i, c][:], in_=g01[i, c][:])
@@ -173,7 +173,7 @@ def tile_picked_ottpolar_none_po_kernel(tc, x_words, x_scales, w1, w2, offs, two
 
         def regroup(u):
             for t in range(2):
-                nc.sync.dma_start(y01[HALF * u : HALF * (u + 1), t, :], y[u][HALF * t : HALF * (t + 1), :])
+                nc.sync.dma_start(y01[HALF * u : HALF * (u + 1), t, :], y[u][t:P:2, :])
 
         vcopy, scopy = nc.vector.tensor_copy, nc.scalar.copy
         pick_words(0)
@@ -193,17 +193,14 @@ def tile_picked_ottpolar_none_po_kernel(tc, x_words, x_scales, w1, w2, offs, two
         cast23(vcopy, 0, 1)
         quant01(0, 1)
         quant23(0)
-        fetch_half(0, 0)
-        fetch_half(0, 1)
-        make_rb_half(0, 0)
+        fetch(0)
+        nc.scalar.activation(sq[0][:], pa_pb[0][:], ACT.Square)
+        make_rb(0)
         cast01(vcopy, 1, 1)
-        make_rb_half(0, 1)
-        open_y(0, "y0")
-        put_rb_half(0, 0)
-        put_rb_half(0, 1)
-        make_sq(0)
-        quant01(1, 1)
         make_ss(0)
+        open_y(0, "y0")
+        put_rb(0)
+        quant01(1, 1)
         product(1, 0)
         product(1, 1)
         root(0, "ra0")

from contextlib import ExitStack

import concourse.mybir as mybir

K, T, S, N, W = 512, 2048, 256, 512, 128
FLOPS = 2 * 2 * K * N * S

F32 = mybir.dt.float32
BF16 = mybir.dt.bfloat16
I32 = mybir.dt.int32
U32 = mybir.dt.uint32
U16 = mybir.dt.uint16
U8 = mybir.dt.uint8
FP8X4 = mybir.dt.float8_e4m3fn_x4
ACT = mybir.ActivationFunctionType
ALU = mybir.AluOpType

P = 128
HALF = 64


def tile_picked_ottpolar_none_po_kernel(tc, x_words, x_scales, w1, w2, offs, two, n1, n2, out_0, out_1, out_2):
    nc = tc.nc
    with ExitStack() as ctx:
        lists = ctx.enter_context(tc.tile_pool(name="lists", bufs=1))
        sb = ctx.enter_context(tc.tile_pool(name="sb", bufs=1))
        psum = ctx.enter_context(tc.psum_pool(name="psum", bufs=1))

        def load_list(name, src):
            tile = lists.tile(list(src.shape), U16, name="list_" + name)
            nc.sync.dma_start(tile[:], src)
            return tile

        raw = {}

        def load_weight(i, c):
            raw[i, c] = sb.tile([P, 4, 256], F32, name="raw%d%d" % (i, c), align_bytes=64)
            nc.sync.dma_start(raw[i, c][:], (w1, w2)[i].rearrange("(p j) n -> p j n", j=4)[:, :, 256 * c : 256 * (c + 1)])

        xs = sb.tile([P, T], U8, name="xs", align_bytes=64)
        xw = sb.tile([P, T], I32, name="xw", align_bytes=64)
        nc.vector.memset(xs[:].bitcast(I32), 0)
        warm = sb.tile([P, 2], F32, name="warm")
        nc.gpsimd.memset(warm[:, 0:1], 1.0)
        nc.scalar.activation(warm[:, 1:2], warm[:, 0:1], ACT.Sqrt)

        def load_words():
            nc.sync.dma_start(xw[:], x_words[0].rearrange("p n t -> p (n t)").bitcast(I32))

        def load_scales(queues):
            for q in range(4):
                queues[q].dma_start(xs[32 * q : 32 * q + 4, :].bitcast(I32), x_scales[0, 4 * q : 4 * q + 4, :].bitcast(I32))

        load_words()
        l_offs = load_list("offs", offs)
        l_two = load_list("two", two)
        load_scales([nc.sync] * 4)
        load_weight(0, 0)
        load_weight(1, 0)
        load_weight(0, 1)
        l_n1 = load_list("n1", n1)
        l_n2 = load_list("n2", n2)
        load_weight(1, 1)

        gw = [sb.tile([P, S], U32, name="gw%d" % i, align_bytes=64) for i in range(2)]
        gs = [sb.tile([P, S], U8, name="gs%d" % i, align_bytes=64) for i in range(2)]

        def pick_words(i):
            nc.vector.tensor_copy(gw[i][:], xw[:].bitcast(U32).indirect((l_offs, l_two)[i][:]))

        def pick_scales(i):
            nc.vector.tensor_copy(gs[i][:], xs[:].indirect((l_offs, l_two)[i][:]))

        g01 = {(i, c): sb.tile([P, 512], BF16, name="g01_%d%d" % (i, c), align_bytes=64) for i in range(2) for c in range(2)}
        g23 = [sb.tile([P, 1024], BF16, name="g23_%d" % i, align_bytes=64) for i in range(2)]
        w01 = {(i, c): sb.tile([P, 128], U32, name="w01_%d%d" % (i, c), align_bytes=64) for i in range(2) for c in range(2)}
        s01 = {(i, c): sb.tile([P, 128], U8, name="s01_%d%d" % (i, c), align_bytes=64) for i in range(2) for c in range(2)}
        w23 = [sb.tile([P, 256], U32, name="w23_%d" % i, align_bytes=64) for i in range(2)]
        s23 = [sb.tile([P, 256], U8, name="s23_%d" % i, align_bytes=64) for i in range(2)]

        def cast01(copy, i, c):
            copy(g01[i, c][:].rearrange("p (m t j) -> p m t j", t=2, j=4),
                 raw[i, c][:].rearrange("p j (m t) -> p m t j", t=4)[:, :, 0:2, :])

        def cast23(copy, i, c):
            copy(g23[i][:].rearrange("p (t c m j) -> p c m t j", t=2, c=2, j=4)[:, c],
                 raw[i, c][:].rearrange("p j (m t) -> p m t j", t=4)[:, :, 2:4, :])

        def quant01(i, c):
            nc.vector.quantize_mx(out=w01[i, c][:].bitcast(FP8X4), scales=s01[i, c][:], in_=g01[i, c][:])

        def quant23(i):
            nc.vector.quantize_mx(out=w23[i][:].bitcast(FP8X4), scales=s23[i][:], in_=g23[i][:])

        banks = [psum.tile([P, S], F32, name="bank%d" % u) for u in range(4)]

        def product(u, i):
            if u < 2:
                words, scales = w01[i, u][:], s01[i, u][:]
            else:
                cols = slice(128 * (u - 2), 128 * (u - 1))
                words, scales = w23[i][:, cols], s23[i][:, cols]
            nc.tensor.matmul_mx(out=banks[u][:], lhsT=words.bitcast(FP8X4), lhsT_scale=scales,
                                rhs=gw[i][:].bitcast(FP8X4), rhs_scale=gs[i][:], start=(i == 0), stop=(i == 1))

        h = {}
        y = {}
        pa_pb, rb, ss, ra = {}, {}, {}, {}
        groups = {0: (0,), 1: (1,), 2: (2, 3)}
        for g, members in groups.items():
            n = len(members)
            pa_pb[g] = sb.tile([P, 2, n * W], F32, name="pair%d" % g, align_bytes=64)
            rb[g] = sb.tile([P, n * W], F32, name="rb%d" % g, align_bytes=64)
            ss[g] = sb.tile([P, n * W], F32, name="ss%d" % g, tag="ss%d" % g, align_bytes=64)

        def place(u):
            g = min(u, 2)
            return g, slice(W * (u - g), W * (u - g + 1))

        def unload(copy, u):
            h[u] = sb.tile([P, S], F32, name="h%d" % u, tag="h%d" % u, align_bytes=64)
            copy(h[u][:], banks[u][:])

        def fetch(u):
            g, cols = place(u)
            nc.scalar.activation(pa_pb[g][:, 0, cols], h[u][:].indirect(l_n1[:]), ACT.Copy)
            nc.scalar.activation(pa_pb[g][:, 1, cols], h[u][:].indirect(l_n2[:]), ACT.Copy)

        def open_y(u, tag):
            y[u] = sb.tile([P, S], F32, name="y%d" % u, tag=tag, align_bytes=64)

        def fetch_half(u, a):
            cols, offsets = slice(HALF * a, HALF * (a + 1)), slice(4 * a, 4 * (a + 1))
            nc.scalar.activation(pa_pb[u][:, 0, cols], h[u][:].indirect(l_n1[:, offsets]), ACT.Copy)
            nc.scalar.activation(pa_pb[u][:, 1, cols], h[u][:].indirect(l_n2[:, offsets]), ACT.Copy)

        def make_rb_half(u, a):
            cols = slice(HALF * a, HALF * (a + 1))
            nc.vector.scalar_tensor_tensor(rb[u][:, cols], pa_pb[u][:, 0, cols], -0.5, pa_pb[u][:, 1, cols], ALU.mult, ALU.add)

        def put_rb_half(u, a):
            cols, offsets = slice(HALF * a, HALF * (a + 1)), slice(4 * a, 4 * (a + 1))
            nc.scalar.activation(y[u][:].indirect(l_n2[:, offsets]), rb[u][:, cols], ACT.Copy)

        def make_rb(u):
            g, cols = place(u)
            nc.vector.scalar_tensor_tensor(rb[g][:, cols], pa_pb[g][:, 0, cols], -0.5, pa_pb[g][:, 1, cols], ALU.mult, ALU.add)

        sq = {g: sb.tile(list(pa_pb[g].shape), F32, name="sq%d" % g, align_bytes=64) for g in groups}

        def make_sq(u):
            g, cols = place(u)
            nc.vector.tensor_tensor(sq[g][:, :, cols], pa_pb[g][:, :, cols], pa_pb[g][:, :, cols], ALU.mult)

        def make_ss(g):
            nc.vector.scalar_tensor_tensor(ss[g][:], sq[g][:, 0, :], 0.25, sq[g][:, 1, :], ALU.add, ALU.add)

        def root(g, tag):
            ra[g] = sb.tile(list(ss[g].shape), F32, name="ra%d" % g, tag=tag, align_bytes=64)
            nc.scalar.activation(ra[g][:], ss[g][:], ACT.Sqrt)

        def put_rb(u):
            g, cols = place(u)
            nc.scalar.activation(y[u][:].indirect(l_n2[:]), rb[g][:, cols], ACT.Copy)

        def put_ra(u):
            g, cols = place(u)
            nc.scalar.activation(y[u][:].indirect(l_n1[:]), ra[g][:, cols], ACT.Copy)

        y01 = sb.tile([P, 2, S], F32, name="y01", align_bytes=64)
        grouped = sb.tile([P, S, 4], BF16, name="grouped", align_bytes=64)
        out_rows = out_0.rearrange("(p t) c -> p t c", t=4)

        def regroup(u):
            for t in range(2):
                nc.sync.dma_start(y01[HALF * u : HALF * (u + 1), t, :], y[u][t:P:2, :])

        vcopy, scopy = nc.vector.tensor_copy, nc.scalar.copy
        pick_words(0)
        pick_words(1)
        pick_scales(0)
        pick_scales(1)
        cast01(scopy, 0, 0)
        cast23(scopy, 0, 0)
        quant01(0, 0)
        cast01(vcopy, 1, 0)
        quant01(1, 0)
        cast23(scopy, 1, 0)
        product(0, 0)
        product(0, 1)
        unload(scopy, 0)
        cast01(vcopy, 0, 1)
        cast23(vcopy, 0, 1)
        quant01(0, 1)
        quant23(0)
        fetch(0)
        nc.scalar.activation(sq[0][:], pa_pb[0][:], ACT.Square)
        make_rb(0)
        cast01(vcopy, 1, 1)
        make_ss(0)
        open_y(0, "y0")
        put_rb(0)
        quant01(1, 1)
        product(1, 0)
        product(1, 1)
        root(0, "ra0")
        put_ra(0)
        regroup(0)
        cast23(vcopy, 1, 1)
        unload(vcopy, 1)
        quant23(1)
        product(2, 0)
        product(2, 1)
        product(3, 0)
        product(3, 1)
        unload(vcopy, 2)
        fetch_half(1, 0)
        fetch_half(1, 1)
        make_rb_half(1, 0)
        unload(vcopy, 3)
        make_rb_half(1, 1)
        open_y(1, "y1")
        put_rb_half(1, 0)
        put_rb_half(1, 1)
        make_sq(1)
        make_ss(1)
        fetch(2)
        root(1, "h2")
        fetch(3)
        make_rb(2)
        make_sq(2)
        put_ra(1)
        regroup(1)
        make_sq(3)
        make_rb(3)
        make_ss(2)
        open_y(2, "h2")
        put_rb(2)
        root(2, "ra2")
        open_y(3, "ss2")
        put_rb(3)
        put_ra(2)
        nc.sync.dma_start(out_rows[:, 0:2, :], y01[:])
        vcopy(grouped[:, :, 0:2], y01[:].rearrange("p t c -> p c t"))
        nc.sync.dma_start(out_rows[:, 2, :], y[2][:])
        vcopy(grouped[:, :, 2], y[2][:])
        put_ra(3)
        nc.sync.dma_start(out_rows[:, 3, :], y[3][:])
        vcopy(grouped[:, :, 3], y[3][:])

        yw = sb.tile([P, S], U32, name="yw", align_bytes=64)
        ys = sb.tile([P, S], U8, name="ys", align_bytes=64)
        nc.vector.quantize_mx(out=yw[:].bitcast(FP8X4), scales=ys[:], in_=grouped[:].rearrange("p c t -> p (c t)"))
        nc.sync.dma_start(out_1[0].rearrange("p n t -> p (n t)").bitcast(I32), yw[:].bitcast(I32))
        for q in range(4):
            queue = nc.scalar if q % 2 == 0 else nc.sync
            queue.dma_start(out_2[0, 4 * q : 4 * q + 4, :].bitcast(I32), ys[32 * q : 32 * q + 4, :].bitcast(I32))
